import numpy as np
import ml_dtypes


def mxq(x, axis, fmt="e4m3"):
    dtype, down = {"e4m3": (ml_dtypes.float8_e4m3fn, 7), "e5m2": (ml_dtypes.float8_e5m2, 14)}[fmt]
    v = np.moveaxis(np.asarray(x, np.float32).astype(ml_dtypes.bfloat16).astype(np.float64), axis, -1)
    blocks = v.reshape(v.shape[:-1] + (-1, 32))
    amax = np.abs(blocks).max(-1, keepdims=True)
    byte = np.maximum(np.where(amax > 0, np.frexp(amax)[1] - 1 + 127, 0) - down, 1)
    scale = np.exp2(byte - 127.0)
    codes = (blocks / scale).astype(np.float32).astype(dtype).astype(np.float64)
    return np.moveaxis((codes * scale).reshape(v.shape), -1, axis)


WIDE = False


def mx_kscale(k):
    if not WIDE:
        return np.ones(k)
    levels = np.array([10, -10, 5, -5, 0])
    if k % 512:
        return np.exp2(np.random.permutation(np.resize(levels, k // 32))).repeat(32)
    a = np.empty((k // 512, 16))
    for p in range(k // 512):
        a[p, :8] = np.random.permutation(np.resize(levels, 8))
        for g in range(8):
            far = levels[np.abs(levels - a[p, g]) >= 10]
            a[p, g + 8] = far[np.random.randint(len(far))]
    return np.exp2(a.ravel()).repeat(32)


def f64(x):
    return np.asarray(x).astype(np.float64)


def striped(idx):
    return np.tile(np.asarray(idx).reshape(-1, 16).T, (8, 1)).astype(np.uint16)


def unstriped(offs):
    return offs[:16].T.reshape(-1).astype(np.int64)


E2M1 = np.array([0.0, 0.5, 1.0, 1.5, 2.0, 3.0, 4.0, 6.0, -0.0, -0.5, -1.0, -1.5, -2.0, -3.0, -4.0, -6.0])


def pack_weight(w, fmt):
    k, n = w.shape
    w = f64(np.asarray(w, np.float32).astype(ml_dtypes.bfloat16)).reshape(k // 32, 32, n)
    amax = np.abs(w).max(1)
    if fmt == "e4m3":
        byte = np.frexp(amax)[1] - 1 + 127 - 7
    else:
        mant, ex = np.frexp(amax / 6.0)
        byte = np.where(mant > 0.5, ex, ex - 1) + 127
    byte = np.clip(np.where(amax > 0, byte, 1), 1, 254)
    scaled = (w * np.exp2(127.0 - byte)[:, None, :]).reshape(k, n).astype(np.float32)
    by_word = np.ascontiguousarray(scaled.reshape(k // 512, 128, 4, n).transpose(0, 1, 3, 2))
    if fmt == "e4m3":
        words = by_word.astype(ml_dtypes.float8_e4m3fn).view(np.uint8)
    else:
        c = by_word.astype(ml_dtypes.float4_e2m1fn).view(np.uint8) & 0xF
        words = (c[..., 0::2] | (c[..., 1::2] << 4)).reshape(k // 512, 128, 2 * n)
    return np.ascontiguousarray(words), np.ascontiguousarray(byte.astype(np.uint8).reshape(k // 512, 16, n))


def unpack_weight(words, scales, fmt):
    g, _, n = scales.shape
    words = np.ascontiguousarray(words).reshape(g, 128, n, -1)
    if fmt == "e4m3":
        vals = words.view(ml_dtypes.float8_e4m3fn).astype(np.float64)
    else:
        nib = np.empty((g, 128, n, 4), np.uint8)
        nib[..., 0::2] = words & 0xF
        nib[..., 1::2] = words >> 4
        vals = E2M1[nib]
    vals = vals * np.repeat(np.exp2(scales.astype(np.float64) - 127.0), 8, axis=1)[..., None]
    return vals.transpose(0, 1, 3, 2).reshape(g * 512, n)


def bf(x):
    return np.asarray(x, np.float32).astype(ml_dtypes.bfloat16)


def planes(Y):
    r, m = Y.shape
    b = f64(bf(Y)).reshape(r // 32, 32, m)
    amax = np.abs(b).max(1)
    byte = np.clip(np.where(amax > 0, np.frexp(amax)[1] - 1 + 127 - 7, 1), 1, 254)
    codes = (b * np.exp2(127.0 - byte)[:, None, :]).reshape(r, m).astype(np.float32).astype(ml_dtypes.float8_e4m3fn).view(np.uint8)
    words = codes.reshape(r // 512, 128, 4, m).transpose(0, 1, 3, 2)
    return np.ascontiguousarray(words), np.ascontiguousarray(byte.astype(np.uint8).reshape(r // 512, 16, m))


D, T, I, J, U, E, M = 512, 2048, 512, 512, 1024, 512, 1024


def setup_inputs():
    n = np.random.standard_normal
    idx = np.random.permutation(T)[:I]
    idx2 = np.random.permutation(U)[:J]
    idx3 = np.random.permutation(U)[:J]
    idx4 = np.random.permutation(M)[:J]
    fd = mx_kscale(D)
    fi = mx_kscale(I)
    ti = np.ones(T)
    ti[idx] = fi
    keysp = pack_weight(n((D, T)) / fd[:, None], "e2m1")
    return {
        "keys_words": keysp[0],
        "keys_scales": keysp[1],
        "notes": (n((D, U)) * 1.0 / np.sqrt(D) * fd[:, None]).astype(np.float32),
        "rowf": (np.random.uniform(0.02, 0.08, (I, 1)) * fi[:, None]).astype(np.float32),
        "vals": (n((E, T)) / ti).astype(np.float32),
        "old": (1.0 * n((E, M))).astype(np.float32),
        "offs": striped(idx),
        "offs2": striped(idx2),
        "offs3": striped(idx3),
        "offs4": striped(idx4),
    }


def reference(keys_words, keys_scales, notes, rowf, vals, old, offs, offs2, offs3, offs4):
    idx = unstriped(offs)
    idx2 = unstriped(offs2)
    idx3 = unstriped(offs3)
    idx4 = unstriped(offs4)
    keysu = unpack_weight(keys_words, keys_scales, "e2m1")
    keysidxg = keysu[:, idx]
    notesq = mxq(f64(notes), 0, "e4m3")
    g1 = keysidxg.T @ notesq
    g9 = g1[:, idx2] - g1[:, idx3]
    g0 = np.maximum(g9, 0.0)
    gr1 = g0 * f64(rowf)
    vt1 = f64(vals)[:, idx].T
    vt1q = mxq(vt1, 0, "e4m3")
    gr1q = mxq(gr1, 0, "e4m3")
    o = vt1q.T @ gr1q
    of = np.zeros((E, M))
    of[:, idx4] = o
    y = f64(old) + of
    words, scales = planes(y)
    return y, words, scales

@@ -1,0 +1,327 @@
+from contextlib import ExitStack
+
+import concourse.mybir as mybir
+from concourse.masks import make_identity
+
+D, T, I, J, U, E, M = 512, 2048, 512, 512, 1024, 512, 1024
+FLOPS = 2 * D * I * U + 2 * I * E * J
+
+F32 = mybir.dt.float32
+BF16 = mybir.dt.bfloat16
+I32 = mybir.dt.int32
+U32 = mybir.dt.uint32
+U16 = mybir.dt.uint16
+U8 = mybir.dt.uint8
+FP8X4 = mybir.dt.float8_e4m3fn_x4
+FP4X4 = mybir.dt.float4_e2m1fn_x4
+ALU = mybir.AluOpType
+COPY = mybir.ActivationFunctionType.Copy
+
+P = 128
+PACK = 4
+BANK = 512
+QUADS = 4
+
+
+def tile_attend_tab_looked_put_pl_kernel(tc, keys_words, keys_scales, notes, rowf, vals, old, offs, offs2, offs3, offs4, out_0, out_1, out_2):
+    nc = tc.nc
+    with ExitStack() as ctx:
+        keep = ctx.enter_context(tc.tile_pool(name="keep", bufs=1))
+        psum = ctx.enter_context(tc.psum_pool(name="psum", bufs=1))
+
+        def sb(name, shape, dtype):
+            return keep.tile(shape, dtype, name=name, align_bytes=64)
+
+        def copy(eng, out, in_):
+            if eng == "v":
+                nc.vector.tensor_copy(out, in_)
+            else:
+                nc.scalar.copy(out, in_)
+
+        def look_up(eng, out, in_):
+            if eng == "v":
+                nc.vector.tensor_copy(out, in_)
+            else:
+                nc.scalar.activation(out, in_, COPY)
+
+        idx = sb("idx", [P, I // 16], U16)
+        idx2 = sb("idx2", [P, J // 16], U16)
+        idx3 = sb("idx3", [P, J // 16], U16)
+        idx4 = sb("idx4", [P, J // 16], U16)
+
+        key_words = sb("key_words", [P, T], U16)
+        key_scales = sb("key_scales", [P, T], U8)
+        chunks = [(0, 256), (256, 256), (512, 256), (768, 256)]
+        notes_raw = [sb("notes_raw%d" % c, [P, PACK, w], F32) for c, (lo, w) in enumerate(chunks)]
+        notes_v = notes.rearrange("(p t) u -> p t u", t=PACK)
+        row_factor = sb("row_factor", [P, PACK], F32)
+        vals_v = vals.rearrange("(p r) t -> r p t", r=PACK)
+        vals_sb = [sb("vals%d" % r, [P, T], F32) for r in range(PACK)]
+        old_v = old.rearrange("(p r) m -> r p m", r=PACK)
+        old_sb = [sb("old%d" % r, [P, M], F32) for r in range(PACK)]
+
+        def load_notes(c):
+            lo, w = chunks[c]
+            nc.sync.dma_start(notes_raw[c][:], notes_v[:, :, lo : lo + w])
+
+        def load_scales(eng, q):
+            eng.dma_start(key_scales[32 * q : 32 * q + 4, :].bitcast(I32), keys_scales[0, 4 * q : 4 * q + 4, :].bitcast(I32))
+
+        def load_scales_wide(eng, q):
+            rows = keys_scales[0, 4 * q : 4 * q + 4, :].bitcast(I32)
+            eng.dma_start(key_scales[32 * q : 32 * (q + 1), :].bitcast(I32), rows.unsqueeze(0).to_broadcast([8, 4, T // 4]))
+
+        nc.sync.dma_start(idx[:], offs)
+        nc.sync.dma_start(key_words[:].bitcast(I32), keys_words[0].bitcast(I32))
+        load_scales_wide(nc.sync, 0)
+        load_scales_wide(nc.sync, 1)
+        load_scales_wide(nc.sync, 2)
+        load_scales_wide(nc.sync, 3)
+        load_notes(0)
+        load_notes(1)
+        load_notes(2)
+        load_notes(3)
+        nc.sync.dma_start(idx3[:], offs3)
+        nc.sync.dma_start(idx2[:], offs2)
+        nc.sync.dma_start(row_factor[:], rowf.rearrange("(p t) o -> p (t o)", t=PACK))
+        nc.sync.dma_start(vals_sb[0][:], vals_v[0])
+        nc.sync.dma_start(idx4[:], offs4)
+        nc.sync.dma_start(vals_sb[1][:], vals_v[1])
+        nc.sync.dma_start(vals_sb[2][:], vals_v[2])
+        nc.sync.dma_start(vals_sb[3][:], vals_v[3])
+        nc.sync.dma_start(old_sb[0][:], old_v[0])
+        nc.sync.dma_start(old_sb[1][:], old_v[1])
+        nc.sync.dma_start(old_sb[2][:], old_v[2])
+        nc.sync.dma_start(old_sb[3][:], old_v[3])
+
+        placed = [sb("placed%d" % r, [P, M], F32) for r in range(PACK)]
+        for r in range(PACK):
+            (nc.vector if r < 4 else nc.gpsimd).memset(placed[r][:], 0.0)
+        ident = sb("ident", [P, P], F32)
+        make_identity(nc, ident[:])
+
+        words_listed = sb("words_listed", [P, I], U16)
+        words_dealt = sb("words_dealt", [P, 2 * I], U8)
+        scales_dealt = sb("scales_dealt", [P, I], U8)
+        nc.vector.tensor_copy(words_listed[:], key_words[:].indirect(idx[:]))
+        nc.vector.tensor_copy(scales_dealt[:].rearrange("p (t m) -> p m t", t=PACK), key_scales[:].indirect(idx[:]))
+        nc.vector.tensor_copy(
+            words_dealt[:].bitcast(U16).rearrange("p (t m) -> p m t", t=PACK),
+            words_listed[:].rearrange("p (m t) -> p m t", t=PACK),
+        )
+
+        scalar_cols = [256, 192, 128, 96]
+        notes_codes = [sb("notes_codes%d" % c, [P, w], U32) for c, (lo, w) in enumerate(chunks)]
+        notes_scales = [sb("notes_scales%d" % c, [P, w], U8) for c, (lo, w) in enumerate(chunks)]
+        g1 = [sb("g1_%d" % t, [P, U], F32) for t in range(PACK)]
+        for c, (lo, w) in enumerate(chunks):
+            woven = sb("notes_woven%d" % c, [P, w, PACK], BF16)
+            src = notes_raw[c][:].rearrange("p t (c i) -> p c t i", i=4)
+            dst = woven[:].rearrange("p (c i) t -> p c t i", i=4)
+            cut = scalar_cols[c] // 4
+            if cut > 0:
+                nc.scalar.copy(dst[:, :cut], src[:, :cut])
+            if cut < w // 4:
+                nc.vector.tensor_copy(dst[:, cut:], src[:, cut:])
+            nc.vector.quantize_mx(out=notes_codes[c][:].bitcast(FP8X4), scales=notes_scales[c][:], in_=woven[:].rearrange("p c t -> p (c t)"))
+
+        banks = {}
+
+        def score(t):
+            for h in range(2):
+                banks[t, h] = psum.tile([P, BANK], F32, name="acc", tag="acc", bufs=6)
+            for c, (lo, w) in enumerate(chunks):
+                nc.tensor.matmul_mx(
+                    out=banks[t, lo // BANK][:, lo % BANK : lo % BANK + w],
+                    lhsT=words_dealt[:, 2 * P * t : 2 * P * (t + 1)].bitcast(FP4X4),
+                    lhsT_scale=scales_dealt[:, P * t : P * (t + 1)],
+                    rhs=notes_codes[c][:].bitcast(FP8X4),
+                    rhs_scale=notes_scales[c][:],
+                    start=True,
+                    stop=True,
+                )
+
+        def drain(eng, t, h):
+            copy(eng, g1[t][:, h * BANK : (h + 1) * BANK], banks[t, h][:])
+
+        table = sb("table", [P, PACK, J], BF16)
+        minus = [sb("minus%d" % t, [P, J], F32) for t in range(PACK)]
+        plus = [sb("plus%d" % t, [P, J], F32) for t in range(PACK)]
+        diff = [sb("diff%d" % t, [P, J], F32) for t in range(PACK)]
+
+        def look_minus(eng, t):
+            look_up(eng, minus[t][:], g1[t][:].indirect(idx3[:]))
+
+        def look_plus(eng, t):
+            look_up(eng, plus[t][:], g1[t][:].indirect(idx2[:]))
+
+        def look_diff(t):
+            nc.vector.tensor_tensor(diff[t][:], g1[t][:].indirect(idx2[:]), minus[t][:], ALU.subtract)
+
+        def sub(eng, t):
+            eng.tensor_tensor(diff[t][:], plus[t][:], minus[t][:], ALU.subtract)
+
+        def weigh(eng, t):
+            eng.tensor_scalar(table[:, t, :], diff[t][:], 0.0, row_factor[:, t : t + 1], ALU.max, ALU.mult)
+
+        table_woven = sb("table_woven", [P, J, PACK], BF16)
+        table_codes = sb("table_codes", [P, J], U32)
+        table_scales = sb("table_scales", [P, J], U8)
+
+        def weave_table(eng, lo, hi):
+            copy(
+                eng,
+                table_woven[:].rearrange("p (c i) t -> p c t i", i=4)[:, lo // 4 : hi // 4],
+                table[:].rearrange("p t (c i) -> p c t i", i=4)[:, lo // 4 : hi // 4],
+            )
+
+        def quant_table():
+            nc.vector.quantize_mx(out=table_codes[:].bitcast(FP8X4), scales=table_scales[:], in_=table_woven[:].rearrange("p c t -> p (c t)"))
+
+        listed = [sb("vals_listed%d" % r, [P, I], BF16) for r in range(PACK)]
+        vals_woven = [sb("vals_woven%d" % r, [P, P * PACK], BF16) for r in range(PACK)]
+        first_codes = sb("vals_codes0", [P, P], U32)
+        later = {}
+
+        def codes_of(r):
+            if r == 0:
+                return first_codes[:]
+            if not later:
+                later[0] = keep.tile([P, PACK - 1, P], U32, name="later_codes", tag="table_woven", align_bytes=64)
+            return later[0][:, r - 1, :]
+
+        vals_scales = [sb("vals_scales%d" % r, [P, P], U8) for r in range(PACK)]
+        turned = {}
+
+        def look_vals(eng, r):
+            look_up(eng, listed[r][:], vals_sb[r][:].indirect(idx[:]))
+            turned[r] = psum.tile([P, 2, P], F32, name="turned", tag="turned", bufs=2)
+            pairs = listed[r][:].bitcast(F32)
+            for u in range(2):
+                nc.tensor.transpose(turned[r][:, u, :], pairs[:, u::2], ident[:])
+
+        def weave_vals(eng, r):
+            copy(eng, vals_woven[r][:].bitcast(F32).rearrange("p (m u) -> p m u", u=2), turned[r][:].rearrange("p u m -> p m u"))
+
+        def quant_vals(r):
+            nc.vector.quantize_mx(out=codes_of(r).bitcast(FP8X4), scales=vals_scales[r][:], in_=vals_woven[r][:])
+
+        result = sb("result", [P, PACK, M], F32)
+        out_v = out_0.rearrange("(p r) m -> r p m", r=PACK)
+        o = [sb("o%d" % r, [P, J], F32) for r in range(PACK)]
+        sums = {}
+
+        def product(r):
+            sums[r] = psum.tile([P, BANK], F32, name="acc", tag="acc", bufs=6)
+            nc.tensor.matmul_mx(
+                out=sums[r][:],
+                lhsT=codes_of(r).bitcast(FP8X4),
+                lhsT_scale=vals_scales[r][:],
+                rhs=table_codes[:].bitcast(FP8X4),
+                rhs_scale=table_scales[:],
+                start=True,
+                stop=True,
+            )
+
+        def fetch(eng, r):
+            copy(eng, o[r][:], sums[r][:])
+
+        def put(eng, r, lo, hi):
+            look_up(eng, placed[r][:].indirect(idx4[:, lo // 16 : hi // 16]), o[r][:, lo:hi])
+
+        def add(eng, r, lo, hi):
+            eng.tensor_tensor(result[:, r, lo:hi], old_sb[r][:, lo:hi], placed[r][:, lo:hi], ALU.add)
+
+        def store(r):
+            nc.sync.dma_start(out_v[r], result[:, r, :])
+
+        out_woven = sb("out_woven", [P, M, PACK], BF16)
+        out_codes = sb("out_codes", [P, M], U32)
+        out_scales = sb("out_scales", [P, M], U8)
+        codes_v = out_1[0].rearrange("p c r -> p (c r)").bitcast(I32)
+
+        def weave_out(eng, lo, hi):
+            copy(
+                eng,
+                out_woven[:].rearrange("p (c i) t -> p c t i", i=4)[:, lo // 4 : hi // 4],
+                result[:].rearrange("p t (c i) -> p c t i", i=4)[:, lo // 4 : hi // 4],
+            )
+
+        def quant_out(lo, hi):
+            nc.vector.quantize_mx(out=out_codes[:, lo:hi].bitcast(FP8X4), scales=out_scales[:, lo:hi], in_=out_woven[:, lo:hi, :].rearrange("p c t -> p (c t)"))
+            nc.sync.dma_start(codes_v[:, lo:hi], out_codes[:, lo:hi].bitcast(I32))
+
+        V, G = nc.vector, nc.gpsimd
+        score(0)
+        score(1)
+        score(2)
+        drain("s",0,0)
+        drain("v",0,1)
+        look_minus("s",0)
+        drain("s",1,0)
+        drain("v",1,1)
+        score(3)
+        look_diff(0)
+        look_minus("s",1)
+        weigh(V,0)
+        drain("s",2,0)
+        drain("s",2,1)
+        look_diff(1)
+        look_minus("s",2)
+        weigh(V,1)
+        drain("s",3,0)
+        drain("s",3,1)
+        look_diff(2)
+        look_minus("s",3)
+        weigh(V,2)
+        look_diff(3)
+        weigh(V,3)
+        look_vals("s",0)
+        weave_vals("s",0)
+        quant_vals(0)
+        weave_table("v",0,512)
+        quant_table()
+        product(0)
+        look_vals("s",1)
+        weave_vals("s",1)
+        quant_vals(1)
+        product(1)
+        look_vals("s",2)
+        weave_vals("s",2)
+        quant_vals(2)
+        product(2)
+        look_vals("s",3)
+        weave_vals("s",3)
+        quant_vals(3)
+        product(3)
+
+        fetch("v",0)
+        put("v",0,0,512)
+        fetch("s",1)
+        fetch("s",2)
+        put("s",1,0,256)
+        put("s",1,256,512)
+        put("v",2,0,512)
+        add(V,0,0,512)
+        add(V,0,512,M)
+        store(0)
+        fetch("s",3)
+        put("s",3,0,256)
+        put("s",3,256,512)
+        add(V,1,0,512)
+        add(V,1,512,M)
+        store(1)
+        add(V,2,0,M)
+        store(2)
+        add(V,3,0,512)
+        weave_out("s",0,320)
+        add(V,3,512,M)
+        store(3)
+        weave_out("v",320,512)
+        quant_out(0,512)
+        weave_out("s",512,768)
+        weave_out("v",768,1024)
+        quant_out(512,1024)
+        for q in range(QUADS):
+            eng = nc.sync if q % 2 == 0 else nc.scalar
+            eng.dma_start(out_2[0, 4 * q : 4 * q + 4, :].bitcast(I32), out_scales[32 * q : 32 * q + 4, :].bitcast(I32))

@@ -21,6 +21,7 @@ P = 128
 PACK = 4
 BANK = 512
 QUADS = 4
+ALIAS = {"vals_woven":"vals3"}
 
 
 def tile_attend_tab_looked_put_pl_kernel(tc, keys_words, keys_scales, notes, rowf, vals, old, offs, offs2, offs3, offs4, out_0, out_1, out_2):
@@ -30,7 +31,7 @@ def tile_attend_tab_looked_put_pl_kernel(tc, keys_words, keys_scales, notes, row
         psum = ctx.enter_context(tc.psum_pool(name="psum", bufs=1))
 
         def sb(name, shape, dtype):
-            return keep.tile(shape, dtype, name=name, align_bytes=64)
+            return keep.tile(shape, dtype, name=name, tag=ALIAS.get(name, name), align_bytes=64)
 
         def copy(eng, out, in_):
             if eng == "v":
@@ -71,13 +72,14 @@ def tile_attend_tab_looked_put_pl_kernel(tc, keys_words, keys_scales, notes, row
             rows = keys_scales[0, 4 * q : 4 * q + 4, :].bitcast(I32)
             eng.dma_start(key_scales[32 * q : 32 * (q + 1), :].bitcast(I32), rows.unsqueeze(0).to_broadcast([8, 4, T // 4]))
 
+        nc.gpsimd.memset(key_scales[:].bitcast(I32), 0)
         nc.sync.dma_start(idx[:], offs)
         nc.sync.dma_start(key_words[:].bitcast(I32), keys_words[0].bitcast(I32))
-        load_scales_wide(nc.sync, 0)
-        load_scales_wide(nc.sync, 1)
-        load_scales_wide(nc.sync, 2)
-        load_scales_wide(nc.sync, 3)
         load_notes(0)
+        load_scales(nc.sync, 0)
+        load_scales(nc.sync, 1)
+        load_scales(nc.sync, 2)
+        load_scales(nc.sync, 3)
         load_notes(1)
         load_notes(2)
         load_notes(3)
@@ -96,7 +98,7 @@ def tile_attend_tab_looked_put_pl_kernel(tc, keys_words, keys_scales, notes, row
 
         placed = [sb("placed%d" % r, [P, M], F32) for r in range(PACK)]
         for r in range(PACK):
-            (nc.vector if r < 4 else nc.gpsimd).memset(placed[r][:], 0.0)
+            (nc.vector if r < 0 else nc.gpsimd).memset(placed[r][:], 0.0)
         ident = sb("ident", [P, P], F32)
         make_identity(nc, ident[:])
 
@@ -106,8 +108,8 @@ def tile_attend_tab_looked_put_pl_kernel(tc, keys_words, keys_scales, notes, row
         nc.vector.tensor_copy(words_listed[:], key_words[:].indirect(idx[:]))
         nc.vector.tensor_copy(scales_dealt[:].rearrange("p (t m) -> p m t", t=PACK), key_scales[:].indirect(idx[:]))
         nc.vector.tensor_copy(
-            words_dealt[:].bitcast(U16).rearrange("p (t m) -> p m t", t=PACK),
-            words_listed[:].rearrange("p (m t) -> p m t", t=PACK),
+            words_dealt[:].bitcast(U16).rearrange("p (t m) -> p t m", t=PACK),
+            words_listed[:].rearrange("p (m t) -> p t m", t=PACK),
         )
 
         scalar_cols = [256, 192, 128, 96]
@@ -129,7 +131,7 @@ def tile_attend_tab_looked_put_pl_kernel(tc, keys_words, keys_scales, notes, row
 
         def score(t):
             for h in range(2):
-                banks[t, h] = psum.tile([P, BANK], F32, name="acc", tag="acc", bufs=6)
+                banks[t, h] = psum.tile([P, BANK], F32, name="acc", tag="acc", bufs=8)
             for c, (lo, w) in enumerate(chunks):
                 nc.tensor.matmul_mx(
                     out=banks[t, lo // BANK][:, lo % BANK : lo % BANK + w],
@@ -179,44 +181,38 @@ def tile_attend_tab_looked_put_pl_kernel(tc, keys_words, keys_scales, notes, row
             nc.vector.quantize_mx(out=table_codes[:].bitcast(FP8X4), scales=table_scales[:], in_=table_woven[:].rearrange("p c t -> p (c t)"))
 
         listed = [sb("vals_listed%d" % r, [P, I], BF16) for r in range(PACK)]
-        vals_woven = [sb("vals_woven%d" % r, [P, P * PACK], BF16) for r in range(PACK)]
-        first_codes = sb("vals_codes0", [P, P], U32)
-        later = {}
-
-        def codes_of(r):
-            if r == 0:
-                return first_codes[:]
-            if not later:
-                later[0] = keep.tile([P, PACK - 1, P], U32, name="later_codes", tag="table_woven", align_bytes=64)
-            return later[0][:, r - 1, :]
-
-        vals_scales = [sb("vals_scales%d" % r, [P, P], U8) for r in range(PACK)]
+        vals_codes = sb("vals_codes", [P, E], U32)
+        vals_scales = sb("vals_scales", [P, E], U8)
         turned = {}
+        vals_woven = []
 
         def look_vals(eng, r):
             look_up(eng, listed[r][:], vals_sb[r][:].indirect(idx[:]))
-            turned[r] = psum.tile([P, 2, P], F32, name="turned", tag="turned", bufs=2)
+            if r % 2 == 0:
+                turned[r // 2] = psum.tile([P, 2, 2, P], F32, name="turned", tag="acc", bufs=8)
             pairs = listed[r][:].bitcast(F32)
             for u in range(2):
-                nc.tensor.transpose(turned[r][:, u, :], pairs[:, u::2], ident[:])
+                nc.tensor.transpose(turned[r // 2][:, r % 2, u, :], pairs[:, u::2], ident[:])
 
-        def weave_vals(eng, r):
-            copy(eng, vals_woven[r][:].bitcast(F32).rearrange("p (m u) -> p m u", u=2), turned[r][:].rearrange("p u m -> p m u"))
+        def weave_vals(eng, g):
+            if g == 0:
+                vals_woven.append(sb("vals_woven", [P, 2, 2 * P * PACK], BF16))
+            copy(eng, vals_woven[0][:, g, :].bitcast(F32).rearrange("p (r m u) -> p r m u", r=2, u=2), turned[g][:].rearrange("p r u m -> p r m u"))
 
-        def quant_vals(r):
-            nc.vector.quantize_mx(out=codes_of(r).bitcast(FP8X4), scales=vals_scales[r][:], in_=vals_woven[r][:])
+        def quant_vals():
+            nc.vector.quantize_mx(out=vals_codes[:].bitcast(FP8X4), scales=vals_scales[:], in_=vals_woven[0][:].rearrange("p g k -> p (g k)"))
 
         result = sb("result", [P, PACK, M], F32)
         out_v = out_0.rearrange("(p r) m -> r p m", r=PACK)
-        o = [sb("o%d" % r, [P, J], F32) for r in range(PACK)]
+        o = {}
         sums = {}
 
         def product(r):
-            sums[r] = psum.tile([P, BANK], F32, name="acc", tag="acc", bufs=6)
+            sums[r] = psum.tile([P, BANK], F32, name="acc", tag="acc", bufs=8)
             nc.tensor.matmul_mx(
                 out=sums[r][:],
-                lhsT=codes_of(r).bitcast(FP8X4),
-                lhsT_scale=vals_scales[r][:],
+                lhsT=vals_codes[:, P * r : P * (r + 1)].bitcast(FP8X4),
+                lhsT_scale=vals_scales[:, P * r : P * (r + 1)],
                 rhs=table_codes[:].bitcast(FP8X4),
                 rhs_scale=table_scales[:],
                 start=True,
@@ -224,6 +220,7 @@ def tile_attend_tab_looked_put_pl_kernel(tc, keys_words, keys_scales, notes, row
             )
 
         def fetch(eng, r):
+            o[r] = sb("o%d" % r, [P, J], F32)
             copy(eng, o[r][:], sums[r][:])
 
         def put(eng, r, lo, hi):
@@ -252,72 +249,61 @@ def tile_attend_tab_looked_put_pl_kernel(tc, keys_words, keys_scales, notes, row
             nc.sync.dma_start(codes_v[:, lo:hi], out_codes[:, lo:hi].bitcast(I32))
 
         V, G = nc.vector, nc.gpsimd
-        score(0)
-        score(1)
-        score(2)
+        for t in range(PACK): score(t)
         drain("s",0,0)
-        drain("v",0,1)
-        look_minus("s",0)
         drain("s",1,0)
-        drain("v",1,1)
-        score(3)
-        look_diff(0)
-        look_minus("s",1)
-        weigh(V,0)
+        drain("s",0,1)
         drain("s",2,0)
-        drain("s",2,1)
-        look_diff(1)
-        look_minus("s",2)
-        weigh(V,1)
         drain("s",3,0)
+        look_minus("s",0)
+        drain("v",1,1)
+        drain("v",2,1)
         drain("s",3,1)
-        look_diff(2)
+        look_minus("s",1)
+        look_minus("s",2)
         look_minus("s",3)
-        weigh(V,2)
+        look_diff(0)
+        look_diff(1)
+        weigh(V,0)
+        look_diff(2)
+        weigh(V,1)
         look_diff(3)
+        weigh(V,2)
         weigh(V,3)
-        look_vals("s",0)
+
+        look_vals("v",0)
+        look_vals("s",1)
+        look_vals("s",2)
+        look_vals("s",3)
         weave_vals("s",0)
-        quant_vals(0)
+        weave_vals("s",1)
         weave_table("v",0,512)
         quant_table()
-        product(0)
-        look_vals("s",1)
-        weave_vals("s",1)
-        quant_vals(1)
-        product(1)
-        look_vals("s",2)
-        weave_vals("s",2)
-        quant_vals(2)
-        product(2)
-        look_vals("s",3)
-        weave_vals("s",3)
-        quant_vals(3)
-        product(3)
+        quant_vals()
+        for r in range(PACK): product(r)
 
         fetch("v",0)
         put("v",0,0,512)
         fetch("s",1)
-        fetch("s",2)
         put("s",1,0,256)
+        fetch("s",2)
         put("s",1,256,512)
-        put("v",2,0,512)
-        add(V,0,0,512)
-        add(V,0,512,M)
+        add(V,0,0,M)
         store(0)
+        add(V,1,0,M)
+        store(1)
+        put("v",2,0,512)
         fetch("s",3)
         put("s",3,0,256)
         put("s",3,256,512)
-        add(V,1,0,512)
-        add(V,1,512,M)
-        store(1)
-        add(V,2,0,M)
-        store(2)
+        add(V,2,0,512)
         add(V,3,0,512)
-        weave_out("s",0,320)
+        weave_out("s",0,288)
+        add(V,2,512,M)
+        store(2)
         add(V,3,512,M)
         store(3)
-        weave_out("v",320,512)
+        weave_out("v",288,512)
         quant_out(0,512)
         weave_out("s",512,768)
         weave_out("v",768,1024)

@@ -98,7 +98,7 @@ def tile_attend_tab_looked_put_pl_kernel(tc, keys_words, keys_scales, notes, row
 
         placed = [sb("placed%d" % r, [P, M], F32) for r in range(PACK)]
         for r in range(PACK):
-            (nc.vector if r < 0 else nc.gpsimd).memset(placed[r][:], 0.0)
+            (nc.vector if r < 3 else nc.gpsimd).memset(placed[r][:], 0.0)
         ident = sb("ident", [P, P], F32)
         make_identity(nc, ident[:])
 
@@ -131,7 +131,7 @@ def tile_attend_tab_looked_put_pl_kernel(tc, keys_words, keys_scales, notes, row
 
         def score(t):
             for h in range(2):
-                banks[t, h] = psum.tile([P, BANK], F32, name="acc", tag="acc", bufs=8)
+                banks[t, h] = psum.tile([P, BANK], F32, name="acc", tag="acc", bufs=6)
             for c, (lo, w) in enumerate(chunks):
                 nc.tensor.matmul_mx(
                     out=banks[t, lo // BANK][:, lo % BANK : lo % BANK + w],
@@ -189,7 +189,7 @@ def tile_attend_tab_looked_put_pl_kernel(tc, keys_words, keys_scales, notes, row
         def look_vals(eng, r):
             look_up(eng, listed[r][:], vals_sb[r][:].indirect(idx[:]))
             if r % 2 == 0:
-                turned[r // 2] = psum.tile([P, 2, 2, P], F32, name="turned", tag="acc", bufs=8)
+                turned[r // 2] = psum.tile([P, 2, 2, P], F32, name="turned", tag="turned", bufs=2)
             pairs = listed[r][:].bitcast(F32)
             for u in range(2):
                 nc.tensor.transpose(turned[r // 2][:, r % 2, u, :], pairs[:, u::2], ident[:])
@@ -208,7 +208,7 @@ def tile_attend_tab_looked_put_pl_kernel(tc, keys_words, keys_scales, notes, row
         sums = {}
 
         def product(r):
-            sums[r] = psum.tile([P, BANK], F32, name="acc", tag="acc", bufs=8)
+            sums[r] = psum.tile([P, BANK], F32, name="acc", tag="acc", bufs=6)
             nc.tensor.matmul_mx(
                 out=sums[r][:],
                 lhsT=vals_codes[:, P * r : P * (r + 1)].bitcast(FP8X4),
@@ -249,17 +249,20 @@ def tile_attend_tab_looked_put_pl_kernel(tc, keys_words, keys_scales, notes, row
             nc.sync.dma_start(codes_v[:, lo:hi], out_codes[:, lo:hi].bitcast(I32))
 
         V, G = nc.vector, nc.gpsimd
-        for t in range(PACK): score(t)
+        score(0)
+        score(1)
+        score(2)
         drain("s",0,0)
         drain("s",1,0)
         drain("s",0,1)
         drain("s",2,0)
-        drain("s",3,0)
         look_minus("s",0)
         drain("v",1,1)
+        score(3)
         drain("v",2,1)
-        drain("s",3,1)
         look_minus("s",1)
+        drain("s",3,0)
+        drain("s",3,1)
         look_minus("s",2)
         look_minus("s",3)
         look_diff(0)
@@ -285,29 +288,29 @@ def tile_attend_tab_looked_put_pl_kernel(tc, keys_words, keys_scales, notes, row
         fetch("v",0)
         put("v",0,0,512)
         fetch("s",1)
-        put("s",1,0,256)
         fetch("s",2)
+        put("s",1,0,256)
         put("s",1,256,512)
-        add(V,0,0,M)
-        store(0)
-        add(V,1,0,M)
-        store(1)
         put("v",2,0,512)
+        add(G,0,0,M)
+        store(0)
         fetch("s",3)
         put("s",3,0,256)
         put("s",3,256,512)
-        add(V,2,0,512)
-        add(V,3,0,512)
-        weave_out("s",0,288)
-        add(V,2,512,M)
+        add(V,1,0,M)
+        store(1)
+        add(V,2,0,M)
         store(2)
-        add(V,3,512,M)
+        add(V,3,0,256)
+        weave_out("s",0,256)
+        add(V,3,256,M)
         store(3)
-        weave_out("v",288,512)
+        weave_out("v",256,512)
         quant_out(0,512)
         weave_out("s",512,768)
         weave_out("v",768,1024)
-        quant_out(512,1024)
+        quant_out(512,768)
+        quant_out(768,1024)
         for q in range(QUADS):
             eng = nc.sync if q % 2 == 0 else nc.scalar
             eng.dma_start(out_2[0, 4 * q : 4 * q + 4, :].bitcast(I32), out_scales[32 * q : 32 * q + 4, :].bitcast(I32))

@@ -18,299 +18,268 @@ ALU = mybir.AluOpType
 COPY = mybir.ActivationFunctionType.Copy
 
 P = 128
-PACK = 4
+PLACES = 4
+QUADRANTS = 4
+PER_COLUMN = 16
 BANK = 512
-QUADS = 4
-ALIAS = {"vals_woven":"vals3"}
+RUN = 4
+CHUNK = 256
+HALF = J // 2
+PRODUCT_BANKS = 6
+GPSIMD_COLUMNS = 384
+QUARTER = M // 4
 
 
-def tile_attend_tab_looked_put_pl_kernel(tc, keys_words, keys_scales, notes, rowf, vals, old, offs, offs2, offs3, offs4, out_0, out_1, out_2):
+def tile_attend_tab_looked_put_pl_kernel(
+    tc, keys_words, keys_scales, notes, rowf, vals, old, offs, offs2, offs3, offs4, out_0, out_1, out_2
+):
     nc = tc.nc
     with ExitStack() as ctx:
-        keep = ctx.enter_context(tc.tile_pool(name="keep", bufs=1))
+        sbuf = ctx.enter_context(tc.tile_pool(name="sbuf", bufs=1))
         psum = ctx.enter_context(tc.psum_pool(name="psum", bufs=1))
 
-        def sb(name, shape, dtype):
-            return keep.tile(shape, dtype, name=name, tag=ALIAS.get(name, name), align_bytes=64)
+        def tile(name, shape, dtype, in_place_of=None):
+            return sbuf.tile(shape, dtype, name=name, tag=in_place_of or name, align_bytes=64)
 
-        def copy(eng, out, in_):
-            if eng == "v":
-                nc.vector.tensor_copy(out, in_)
-            else:
-                nc.scalar.copy(out, in_)
+        def product_bank(columns):
+            return psum.tile([P, columns], F32, name="product", tag="product", bufs=PRODUCT_BANKS)
 
-        def look_up(eng, out, in_):
-            if eng == "v":
-                nc.vector.tensor_copy(out, in_)
-            else:
-                nc.scalar.activation(out, in_, COPY)
+        def scalar_indirect(out, in_):
+            nc.scalar.activation(out, in_, COPY)
 
-        idx = sb("idx", [P, I // 16], U16)
-        idx2 = sb("idx2", [P, J // 16], U16)
-        idx3 = sb("idx3", [P, J // 16], U16)
-        idx4 = sb("idx4", [P, J // 16], U16)
+        def weave(copy, woven, rows):
+            copy(woven.rearrange("p (c i) t -> p c t i", i=RUN), rows.rearrange("p t (c i) -> p c t i", i=RUN))
 
-        key_words = sb("key_words", [P, T], U16)
-        key_scales = sb("key_scales", [P, T], U8)
-        chunks = [(0, 256), (256, 256), (512, 256), (768, 256)]
-        notes_raw = [sb("notes_raw%d" % c, [P, PACK, w], F32) for c, (lo, w) in enumerate(chunks)]
-        notes_v = notes.rearrange("(p t) u -> p t u", t=PACK)
-        row_factor = sb("row_factor", [P, PACK], F32)
-        vals_v = vals.rearrange("(p r) t -> r p t", r=PACK)
-        vals_sb = [sb("vals%d" % r, [P, T], F32) for r in range(PACK)]
-        old_v = old.rearrange("(p r) m -> r p m", r=PACK)
-        old_sb = [sb("old%d" % r, [P, M], F32) for r in range(PACK)]
+        def quantize(codes, scales, woven):
+            nc.vector.quantize_mx(out=codes.bitcast(FP8X4), scales=scales, in_=woven)
 
-        def load_notes(c):
-            lo, w = chunks[c]
-            nc.sync.dma_start(notes_raw[c][:], notes_v[:, :, lo : lo + w])
-
-        def load_scales(eng, q):
-            eng.dma_start(key_scales[32 * q : 32 * q + 4, :].bitcast(I32), keys_scales[0, 4 * q : 4 * q + 4, :].bitcast(I32))
-
-        def load_scales_wide(eng, q):
-            rows = keys_scales[0, 4 * q : 4 * q + 4, :].bitcast(I32)
-            eng.dma_start(key_scales[32 * q : 32 * (q + 1), :].bitcast(I32), rows.unsqueeze(0).to_broadcast([8, 4, T // 4]))
-
-        nc.gpsimd.memset(key_scales[:].bitcast(I32), 0)
-        nc.sync.dma_start(idx[:], offs)
-        nc.sync.dma_start(key_words[:].bitcast(I32), keys_words[0].bitcast(I32))
-        load_notes(0)
-        load_scales(nc.sync, 0)
-        load_scales(nc.sync, 1)
-        load_scales(nc.sync, 2)
-        load_scales(nc.sync, 3)
-        load_notes(1)
-        load_notes(2)
-        load_notes(3)
-        nc.sync.dma_start(idx3[:], offs3)
-        nc.sync.dma_start(idx2[:], offs2)
-        nc.sync.dma_start(row_factor[:], rowf.rearrange("(p t) o -> p (t o)", t=PACK))
-        nc.sync.dma_start(vals_sb[0][:], vals_v[0])
-        nc.sync.dma_start(idx4[:], offs4)
-        nc.sync.dma_start(vals_sb[1][:], vals_v[1])
-        nc.sync.dma_start(vals_sb[2][:], vals_v[2])
-        nc.sync.dma_start(vals_sb[3][:], vals_v[3])
-        nc.sync.dma_start(old_sb[0][:], old_v[0])
-        nc.sync.dma_start(old_sb[1][:], old_v[1])
-        nc.sync.dma_start(old_sb[2][:], old_v[2])
-        nc.sync.dma_start(old_sb[3][:], old_v[3])
-
-        placed = [sb("placed%d" % r, [P, M], F32) for r in range(PACK)]
-        for r in range(PACK):
-            (nc.vector if r < 3 else nc.gpsimd).memset(placed[r][:], 0.0)
-        ident = sb("ident", [P, P], F32)
-        make_identity(nc, ident[:])
-
-        words_listed = sb("words_listed", [P, I], U16)
-        words_dealt = sb("words_dealt", [P, 2 * I], U8)
-        scales_dealt = sb("scales_dealt", [P, I], U8)
-        nc.vector.tensor_copy(words_listed[:], key_words[:].indirect(idx[:]))
-        nc.vector.tensor_copy(scales_dealt[:].rearrange("p (t m) -> p m t", t=PACK), key_scales[:].indirect(idx[:]))
-        nc.vector.tensor_copy(
-            words_dealt[:].bitcast(U16).rearrange("p (t m) -> p t m", t=PACK),
-            words_listed[:].rearrange("p (m t) -> p t m", t=PACK),
-        )
-
-        scalar_cols = [256, 192, 128, 96]
-        notes_codes = [sb("notes_codes%d" % c, [P, w], U32) for c, (lo, w) in enumerate(chunks)]
-        notes_scales = [sb("notes_scales%d" % c, [P, w], U8) for c, (lo, w) in enumerate(chunks)]
-        g1 = [sb("g1_%d" % t, [P, U], F32) for t in range(PACK)]
-        for c, (lo, w) in enumerate(chunks):
-            woven = sb("notes_woven%d" % c, [P, w, PACK], BF16)
-            src = notes_raw[c][:].rearrange("p t (c i) -> p c t i", i=4)
-            dst = woven[:].rearrange("p (c i) t -> p c t i", i=4)
-            cut = scalar_cols[c] // 4
-            if cut > 0:
-                nc.scalar.copy(dst[:, :cut], src[:, :cut])
-            if cut < w // 4:
-                nc.vector.tensor_copy(dst[:, cut:], src[:, cut:])
-            nc.vector.quantize_mx(out=notes_codes[c][:].bitcast(FP8X4), scales=notes_scales[c][:], in_=woven[:].rearrange("p c t -> p (c t)"))
-
-        banks = {}
-
-        def score(t):
-            for h in range(2):
-                banks[t, h] = psum.tile([P, BANK], F32, name="acc", tag="acc", bufs=6)
-            for c, (lo, w) in enumerate(chunks):
-                nc.tensor.matmul_mx(
-                    out=banks[t, lo // BANK][:, lo % BANK : lo % BANK + w],
-                    lhsT=words_dealt[:, 2 * P * t : 2 * P * (t + 1)].bitcast(FP4X4),
-                    lhsT_scale=scales_dealt[:, P * t : P * (t + 1)],
-                    rhs=notes_codes[c][:].bitcast(FP8X4),
-                    rhs_scale=notes_scales[c][:],
-                    start=True,
-                    stop=True,
-                )
-
-        def drain(eng, t, h):
-            copy(eng, g1[t][:, h * BANK : (h + 1) * BANK], banks[t, h][:])
-
-        table = sb("table", [P, PACK, J], BF16)
-        minus = [sb("minus%d" % t, [P, J], F32) for t in range(PACK)]
-        plus = [sb("plus%d" % t, [P, J], F32) for t in range(PACK)]
-        diff = [sb("diff%d" % t, [P, J], F32) for t in range(PACK)]
-
-        def look_minus(eng, t):
-            look_up(eng, minus[t][:], g1[t][:].indirect(idx3[:]))
-
-        def look_plus(eng, t):
-            look_up(eng, plus[t][:], g1[t][:].indirect(idx2[:]))
-
-        def look_diff(t):
-            nc.vector.tensor_tensor(diff[t][:], g1[t][:].indirect(idx2[:]), minus[t][:], ALU.subtract)
-
-        def sub(eng, t):
-            eng.tensor_tensor(diff[t][:], plus[t][:], minus[t][:], ALU.subtract)
-
-        def weigh(eng, t):
-            eng.tensor_scalar(table[:, t, :], diff[t][:], 0.0, row_factor[:, t : t + 1], ALU.max, ALU.mult)
-
-        table_woven = sb("table_woven", [P, J, PACK], BF16)
-        table_codes = sb("table_codes", [P, J], U32)
-        table_scales = sb("table_scales", [P, J], U8)
-
-        def weave_table(eng, lo, hi):
-            copy(
-                eng,
-                table_woven[:].rearrange("p (c i) t -> p c t i", i=4)[:, lo // 4 : hi // 4],
-                table[:].rearrange("p t (c i) -> p c t i", i=4)[:, lo // 4 : hi // 4],
-            )
-
-        def quant_table():
-            nc.vector.quantize_mx(out=table_codes[:].bitcast(FP8X4), scales=table_scales[:], in_=table_woven[:].rearrange("p c t -> p (c t)"))
-
-        listed = [sb("vals_listed%d" % r, [P, I], BF16) for r in range(PACK)]
-        vals_codes = sb("vals_codes", [P, E], U32)
-        vals_scales = sb("vals_scales", [P, E], U8)
-        turned = {}
-        vals_woven = []
-
-        def look_vals(eng, r):
-            look_up(eng, listed[r][:], vals_sb[r][:].indirect(idx[:]))
-            if r % 2 == 0:
-                turned[r // 2] = psum.tile([P, 2, 2, P], F32, name="turned", tag="turned", bufs=2)
-            pairs = listed[r][:].bitcast(F32)
-            for u in range(2):
-                nc.tensor.transpose(turned[r // 2][:, r % 2, u, :], pairs[:, u::2], ident[:])
-
-        def weave_vals(eng, g):
-            if g == 0:
-                vals_woven.append(sb("vals_woven", [P, 2, 2 * P * PACK], BF16))
-            copy(eng, vals_woven[0][:, g, :].bitcast(F32).rearrange("p (r m u) -> p r m u", r=2, u=2), turned[g][:].rearrange("p r u m -> p r m u"))
-
-        def quant_vals():
-            nc.vector.quantize_mx(out=vals_codes[:].bitcast(FP8X4), scales=vals_scales[:], in_=vals_woven[0][:].rearrange("p g k -> p (g k)"))
-
-        result = sb("result", [P, PACK, M], F32)
-        out_v = out_0.rearrange("(p r) m -> r p m", r=PACK)
-        o = {}
-        sums = {}
-
-        def product(r):
-            sums[r] = psum.tile([P, BANK], F32, name="acc", tag="acc", bufs=6)
+        def multiply(out, stationary, stationary_scales, codes, scales):
             nc.tensor.matmul_mx(
-                out=sums[r][:],
-                lhsT=vals_codes[:, P * r : P * (r + 1)].bitcast(FP8X4),
-                lhsT_scale=vals_scales[:, P * r : P * (r + 1)],
-                rhs=table_codes[:].bitcast(FP8X4),
-                rhs_scale=table_scales[:],
+                out=out,
+                lhsT=stationary,
+                lhsT_scale=stationary_scales,
+                rhs=codes.bitcast(FP8X4),
+                rhs_scale=scales,
                 start=True,
                 stop=True,
             )
 
-        def fetch(eng, r):
-            o[r] = sb("o%d" % r, [P, J], F32)
-            copy(eng, o[r][:], sums[r][:])
+        idx = tile("idx", [P, I // PER_COLUMN], U16)
+        idx2 = tile("idx2", [P, J // PER_COLUMN], U16)
+        idx3 = tile("idx3", [P, J // PER_COLUMN], U16)
+        idx4 = tile("idx4", [P, J // PER_COLUMN], U16)
+        key_words = tile("key_words", [P, T], U16)
+        key_scales = tile("key_scales", [P, T], U8)
+        chunks = U // CHUNK
+        notes_rows = [tile("notes_rows%d" % c, [P, PLACES, CHUNK], F32) for c in range(chunks)]
+        row_factor = tile("row_factor", [P, PLACES], F32)
+        vals_rows = [tile("vals_rows%d" % r, [P, T], F32) for r in range(PLACES)]
+        old_rows = [tile("old_rows%d" % r, [P, M], F32) for r in range(PLACES)]
+        notes_dealt = notes.rearrange("(p t) u -> p t u", t=PLACES)
+        vals_dealt = vals.rearrange("(p r) t -> r p t", r=PLACES)
+        old_dealt = old.rearrange("(p r) m -> r p m", r=PLACES)
+        out_dealt = out_0.rearrange("(p r) m -> r p m", r=PLACES)
 
-        def put(eng, r, lo, hi):
-            look_up(eng, placed[r][:].indirect(idx4[:, lo // 16 : hi // 16]), o[r][:, lo:hi])
+        nc.gpsimd.memset(key_scales[:].bitcast(I32), 0)
+        nc.sync.dma_start(idx[:], offs)
+        nc.sync.dma_start(key_words[:].bitcast(I32), keys_words[0].bitcast(I32))
+        nc.sync.dma_start(notes_rows[0][:], notes_dealt[:, :, :CHUNK])
+        for q in range(QUADRANTS):
+            nc.sync.dma_start(
+                key_scales[32 * q : 32 * q + 4, :].bitcast(I32), keys_scales[0, 4 * q : 4 * q + 4, :].bitcast(I32)
+            )
+        for c in range(1, chunks):
+            nc.sync.dma_start(notes_rows[c][:], notes_dealt[:, :, CHUNK * c : CHUNK * (c + 1)])
+        nc.sync.dma_start(idx3[:], offs3)
+        nc.sync.dma_start(idx2[:], offs2)
+        nc.sync.dma_start(row_factor[:], rowf.rearrange("(p t) o -> p (t o)", t=PLACES))
+        nc.sync.dma_start(vals_rows[0][:], vals_dealt[0])
+        nc.sync.dma_start(idx4[:], offs4)
+        for r in range(1, PLACES):
+            nc.sync.dma_start(vals_rows[r][:], vals_dealt[r])
+        for r in range(PLACES):
+            nc.sync.dma_start(old_rows[r][:], old_dealt[r])
 
-        def add(eng, r, lo, hi):
-            eng.tensor_tensor(result[:, r, lo:hi], old_sb[r][:, lo:hi], placed[r][:, lo:hi], ALU.add)
+        placed = [tile("placed%d" % r, [P, M], F32) for r in range(PLACES)]
+        for r in range(PLACES - 1):
+            nc.vector.memset(placed[r][:], 0.0)
+        nc.gpsimd.memset(placed[PLACES - 1][:], 0.0)
+        identity = tile("identity", [P, P], F32)
+        make_identity(nc, identity[:])
 
-        def store(r):
-            nc.sync.dma_start(out_v[r], result[:, r, :])
+        words_listed = tile("words_listed", [P, I], U16)
+        words_dealt = tile("words_dealt", [P, 2 * I], U8)
+        scales_dealt = tile("scales_dealt", [P, I], U8)
+        nc.vector.tensor_copy(words_listed[:], key_words[:].indirect(idx[:]))
+        nc.vector.tensor_copy(scales_dealt[:].rearrange("p (t m) -> p m t", t=PLACES), key_scales[:].indirect(idx[:]))
+        nc.vector.tensor_copy(
+            words_dealt[:].bitcast(U16).rearrange("p (t m) -> p t m", t=PLACES),
+            words_listed[:].rearrange("p (m t) -> p t m", t=PLACES),
+        )
 
-        out_woven = sb("out_woven", [P, M, PACK], BF16)
-        out_codes = sb("out_codes", [P, M], U32)
-        out_scales = sb("out_scales", [P, M], U8)
-        codes_v = out_1[0].rearrange("p c r -> p (c r)").bitcast(I32)
+        notes_codes = [tile("notes_codes%d" % c, [P, CHUNK], U32) for c in range(chunks)]
+        notes_scales = [tile("notes_scales%d" % c, [P, CHUNK], U8) for c in range(chunks)]
+        for c in range(chunks):
+            notes_woven = tile("notes_woven%d" % c, [P, CHUNK, PLACES], BF16)
+            weave(nc.scalar.copy if c < chunks // 2 else nc.vector.tensor_copy, notes_woven[:], notes_rows[c][:])
+            quantize(notes_codes[c][:], notes_scales[c][:], notes_woven[:].rearrange("p c t -> p (c t)"))
 
-        def weave_out(eng, lo, hi):
-            copy(
-                eng,
-                out_woven[:].rearrange("p (c i) t -> p c t i", i=4)[:, lo // 4 : hi // 4],
-                result[:].rearrange("p t (c i) -> p c t i", i=4)[:, lo // 4 : hi // 4],
+        g1 = [tile("g1_%d" % t, [P, U], F32) for t in range(PLACES)]
+        score_banks = {}
+
+        def score(t):
+            for side in range(U // BANK):
+                score_banks[t, side] = product_bank(BANK)
+            for c in range(chunks):
+                side, first = divmod(CHUNK * c, BANK)
+                multiply(
+                    score_banks[t, side][:, first : first + CHUNK],
+                    words_dealt[:, 2 * P * t : 2 * P * (t + 1)].bitcast(FP4X4),
+                    scales_dealt[:, P * t : P * (t + 1)],
+                    notes_codes[c][:],
+                    notes_scales[c][:],
+                )
+
+        def empty(copy, t, side):
+            copy(g1[t][:, BANK * side : BANK * (side + 1)], score_banks[t, side][:])
+
+        for t in range(PLACES - 1):
+            score(t)
+        for t in range(PLACES - 1):
+            empty(nc.scalar.copy, t, 0)
+        for t in range(2):
+            empty(nc.scalar.copy, t, 1)
+        score(PLACES - 1)
+        for t, side in ((2, 1), (3, 0), (3, 1)):
+            empty(nc.vector.tensor_copy, t, side)
+
+        turned = [psum.tile([P, 2, 2, P], F32, name="turned%d" % g) for g in range(PLACES // 2)]
+
+        def look_up_values(copy, r):
+            vals_listed = tile("vals_listed%d" % r, [P, I], BF16)
+            copy(vals_listed[:], vals_rows[r][:].indirect(idx[:]))
+            for u in range(2):
+                nc.tensor.transpose(turned[r // 2][:, r % 2, u, :], vals_listed[:].bitcast(F32)[:, u::2], identity[:])
+
+        subtrahend = [tile("subtrahend%d" % t, [P, J], F32) for t in range(PLACES)]
+        for t in range(PLACES):
+            scalar_indirect(subtrahend[t][:], g1[t][:].indirect(idx3[:]))
+        look_up_values(nc.vector.tensor_copy, 0)
+        difference = tile("difference", [P, PLACES, J], F32, in_place_of="vals_rows0")
+        table = tile("table", [P, PLACES, J], BF16)
+
+        def subtract(t):
+            nc.vector.tensor_tensor(difference[:, t, :], g1[t][:].indirect(idx2[:]), subtrahend[t][:], ALU.subtract)
+
+        def weigh(t):
+            nc.vector.tensor_scalar(table[:, t, :], difference[:, t, :], 0.0, row_factor[:, t : t + 1], ALU.max, ALU.mult)
+
+        subtract(0)
+        for t in range(1, PLACES):
+            subtract(t)
+            weigh(t - 1)
+        weigh(PLACES - 1)
+        for r in range(1, PLACES):
+            look_up_values(scalar_indirect, r)
+
+        table_codes = [tile("table_codes%d" % h, [P, HALF], U32) for h in range(2)]
+        table_scales = [tile("table_scales%d" % h, [P, HALF], U8) for h in range(2)]
+        first_woven = tile("first_woven", [P, HALF, PLACES], BF16)
+        weave(nc.vector.tensor_copy, first_woven[:], table[:, :, :HALF])
+        quantize(table_codes[0][:], table_scales[0][:], first_woven[:].rearrange("p c t -> p (c t)"))
+
+        vals_woven = tile("vals_woven", [P, PLACES // 2, 2 * P * PLACES], BF16, in_place_of="vals_rows3")
+        for g in range(PLACES // 2):
+            nc.scalar.copy(
+                vals_woven[:, g, :].bitcast(F32).rearrange("p (r m u) -> p r m u", r=2, u=2),
+                turned[g][:].rearrange("p r u m -> p r m u"),
+            )
+        second_woven = tile("second_woven", [P, HALF, PLACES], BF16, in_place_of="vals_listed3")
+        weave(nc.scalar.copy, second_woven[:], table[:, :, HALF:])
+        vals_codes = tile("vals_codes", [P, E], U32)
+        vals_scales = tile("vals_scales", [P, E], U8)
+        quantize(vals_codes[:], vals_scales[:], vals_woven[:].rearrange("p g k -> p (g k)"))
+
+        sum_banks = {}
+
+        def product(r, h):
+            if r < 2:
+                sum_banks[r, h] = product_bank(HALF)
+                target = sum_banks[r, h][:]
+            else:
+                if h == 0:
+                    sum_banks[r] = product_bank(J)
+                target = sum_banks[r][:, HALF * h : HALF * (h + 1)]
+            multiply(
+                target,
+                vals_codes[:, P * r : P * (r + 1)].bitcast(FP8X4),
+                vals_scales[:, P * r : P * (r + 1)],
+                table_codes[h][:],
+                table_scales[h][:],
             )
 
-        def quant_out(lo, hi):
-            nc.vector.quantize_mx(out=out_codes[:, lo:hi].bitcast(FP8X4), scales=out_scales[:, lo:hi], in_=out_woven[:, lo:hi, :].rearrange("p c t -> p (c t)"))
-            nc.sync.dma_start(codes_v[:, lo:hi], out_codes[:, lo:hi].bitcast(I32))
+        for r in range(PLACES):
+            product(r, 0)
+        quantize(table_codes[1][:], table_scales[1][:], second_woven[:].rearrange("p c t -> p (c t)"))
+        for r in range(PLACES):
+            product(r, 1)
 
-        V, G = nc.vector, nc.gpsimd
-        score(0)
-        score(1)
-        score(2)
-        drain("s",0,0)
-        drain("s",1,0)
-        drain("s",0,1)
-        drain("s",2,0)
-        look_minus("s",0)
-        drain("v",1,1)
-        score(3)
-        drain("v",2,1)
-        look_minus("s",1)
-        drain("s",3,0)
-        drain("s",3,1)
-        look_minus("s",2)
-        look_minus("s",3)
-        look_diff(0)
-        look_diff(1)
-        weigh(V,0)
-        look_diff(2)
-        weigh(V,1)
-        look_diff(3)
-        weigh(V,2)
-        weigh(V,3)
+        o = [tile("o%d" % r, [P, J], F32) for r in range(PLACES)]
+        result = tile("result", [P, PLACES, M], F32)
 
-        look_vals("v",0)
-        look_vals("s",1)
-        look_vals("s",2)
-        look_vals("s",3)
-        weave_vals("s",0)
-        weave_vals("s",1)
-        weave_table("v",0,512)
-        quant_table()
-        quant_vals()
-        for r in range(PACK): product(r)
+        def scatter(copy, r, first, last):
+            copy(placed[r][:].indirect(idx4[:, first // PER_COLUMN : last // PER_COLUMN]), o[r][:, first:last])
 
-        fetch("v",0)
-        put("v",0,0,512)
-        fetch("s",1)
-        fetch("s",2)
-        put("s",1,0,256)
-        put("s",1,256,512)
-        put("v",2,0,512)
-        add(G,0,0,M)
+        def add(engine, r, first, last):
+            engine.tensor_tensor(result[:, r, first:last], old_rows[r][:, first:last], placed[r][:, first:last], ALU.add)
+
+        def store(r):
+            nc.sync.dma_start(out_dealt[r], result[:, r, :])
+
+        nc.vector.tensor_copy(o[0][:, :HALF], sum_banks[0, 0][:])
+        scatter(nc.vector.tensor_copy, 0, 0, HALF)
+        nc.scalar.copy(o[1][:, :HALF], sum_banks[1, 0][:])
+        scatter(scalar_indirect, 1, 0, HALF)
+        nc.vector.tensor_copy(o[0][:, HALF:], sum_banks[0, 1][:])
+        scatter(nc.vector.tensor_copy, 0, HALF, J)
+        nc.scalar.copy(o[1][:, HALF:], sum_banks[1, 1][:])
+        nc.scalar.copy(o[2][:], sum_banks[2][:])
+        scatter(scalar_indirect, 1, HALF, J)
+        scatter(nc.vector.tensor_copy, 2, 0, J)
+        add(nc.gpsimd, 0, 0, M)
         store(0)
-        fetch("s",3)
-        put("s",3,0,256)
-        put("s",3,256,512)
-        add(V,1,0,M)
+        nc.scalar.copy(o[3][:], sum_banks[3][:])
+        for h in range(2):
+            scatter(scalar_indirect, 3, HALF * h, HALF * (h + 1))
+        add(nc.gpsimd, 1, 0, GPSIMD_COLUMNS)
+        add(nc.vector, 1, GPSIMD_COLUMNS, M)
         store(1)
-        add(V,2,0,M)
+        add(nc.vector, 2, 0, M)
         store(2)
-        add(V,3,0,256)
-        weave_out("s",0,256)
-        add(V,3,256,M)
+
+        out_woven = tile("out_woven", [P, M, PLACES], BF16)
+        out_codes = tile("out_codes", [P, M], U32)
+        out_scales = tile("out_scales", [P, M], U8)
+        words_out = out_1[0].rearrange("p c r -> p (c r)").bitcast(I32)
+
+        def weave_result(copy, quarter):
+            columns = slice(QUARTER * quarter, QUARTER * (quarter + 1))
+            weave(copy, out_woven[:, columns, :], result[:, :, columns])
+
+        def hand_on(first, last):
+            quantize(out_codes[:, first:last], out_scales[:, first:last], out_woven[:, first:last, :].rearrange("p c t -> p (c t)"))
+            nc.sync.dma_start(words_out[:, first:last], out_codes[:, first:last].bitcast(I32))
+
+        add(nc.vector, 3, 0, QUARTER)
+        weave_result(nc.scalar.copy, 0)
+        add(nc.vector, 3, QUARTER, M)
         store(3)
-        weave_out("v",256,512)
-        quant_out(0,512)
-        weave_out("s",512,768)
-        weave_out("v",768,1024)
-        quant_out(512,768)
-        quant_out(768,1024)
-        for q in range(QUADS):
-            eng = nc.sync if q % 2 == 0 else nc.scalar
-            eng.dma_start(out_2[0, 4 * q : 4 * q + 4, :].bitcast(I32), out_scales[32 * q : 32 * q + 4, :].bitcast(I32))
+        weave_result(nc.vector.tensor_copy, 1)
+        hand_on(0, 2 * QUARTER)
+        weave_result(nc.scalar.copy, 2)
+        weave_result(nc.vector.tensor_copy, 3)
+        hand_on(2 * QUARTER, 3 * QUARTER)
+        hand_on(3 * QUARTER, M)
+        for q in range(QUADRANTS):
+            queue = nc.sync if q % 2 == 0 else nc.scalar
+            queue.dma_start(out_2[0, 4 * q : 4 * q + 4, :].bitcast(I32), out_scales[32 * q : 32 * q + 4, :].bitcast(I32))

@@ -26,7 +26,7 @@ RUN = 4
 CHUNK = 256
 HALF = J // 2
 PRODUCT_BANKS = 6
-GPSIMD_COLUMNS = 384
+SCALAR_ENTRIES = 128
 QUARTER = M // 4
 
 
@@ -230,8 +230,8 @@ def tile_attend_tab_looked_put_pl_kernel(
         def scatter(copy, r, first, last):
             copy(placed[r][:].indirect(idx4[:, first // PER_COLUMN : last // PER_COLUMN]), o[r][:, first:last])
 
-        def add(engine, r, first, last):
-            engine.tensor_tensor(result[:, r, first:last], old_rows[r][:, first:last], placed[r][:, first:last], ALU.add)
+        def add(r, first, last):
+            nc.vector.tensor_tensor(result[:, r, first:last], old_rows[r][:, first:last], placed[r][:, first:last], ALU.add)
 
         def store(r):
             nc.sync.dma_start(out_dealt[r], result[:, r, :])
@@ -245,16 +245,17 @@ def tile_attend_tab_looked_put_pl_kernel(
         nc.scalar.copy(o[1][:, HALF:], sum_banks[1, 1][:])
         nc.scalar.copy(o[2][:], sum_banks[2][:])
         scatter(scalar_indirect, 1, HALF, J)
-        scatter(nc.vector.tensor_copy, 2, 0, J)
-        add(nc.gpsimd, 0, 0, M)
+        scatter(scalar_indirect, 2, 0, SCALAR_ENTRIES)
+        add(0, 0, M)
         store(0)
+        add(1, 0, M // 2)
+        scatter(nc.vector.tensor_copy, 2, SCALAR_ENTRIES, J)
+        add(1, M // 2, M)
+        store(1)
         nc.scalar.copy(o[3][:], sum_banks[3][:])
         for h in range(2):
             scatter(scalar_indirect, 3, HALF * h, HALF * (h + 1))
-        add(nc.gpsimd, 1, 0, GPSIMD_COLUMNS)
-        add(nc.vector, 1, GPSIMD_COLUMNS, M)
-        store(1)
-        add(nc.vector, 2, 0, M)
+        add(2, 0, M)
         store(2)
 
         out_woven = tile("out_woven", [P, M, PLACES], BF16)
@@ -270,9 +271,9 @@ def tile_attend_tab_looked_put_pl_kernel(
             quantize(out_codes[:, first:last], out_scales[:, first:last], out_woven[:, first:last, :].rearrange("p c t -> p (c t)"))
             nc.sync.dma_start(words_out[:, first:last], out_codes[:, first:last].bitcast(I32))
 
-        add(nc.vector, 3, 0, QUARTER)
+        add(3, 0, QUARTER)
         weave_result(nc.scalar.copy, 0)
-        add(nc.vector, 3, QUARTER, M)
+        add(3, QUARTER, M)
         store(3)
         weave_result(nc.vector.tensor_copy, 1)
         hand_on(0, 2 * QUARTER)

from contextlib import ExitStack

import concourse.mybir as mybir
from concourse.masks import make_identity

D, T, I, J, U, E, M = 512, 2048, 512, 512, 1024, 512, 1024
FLOPS = 2 * D * I * U + 2 * I * E * J

F32 = mybir.dt.float32
BF16 = mybir.dt.bfloat16
I32 = mybir.dt.int32
U32 = mybir.dt.uint32
U16 = mybir.dt.uint16
U8 = mybir.dt.uint8
FP8X4 = mybir.dt.float8_e4m3fn_x4
FP4X4 = mybir.dt.float4_e2m1fn_x4
ALU = mybir.AluOpType
COPY = mybir.ActivationFunctionType.Copy

P = 128
PLACES = 4
QUADRANTS = 4
PER_COLUMN = 16
BANK = 512
RUN = 4
CHUNK = 256
HALF = J // 2
PRODUCT_BANKS = 6
SCALAR_ENTRIES = 128
QUARTER = M // 4


def tile_attend_tab_looked_put_pl_kernel(
    tc, keys_words, keys_scales, notes, rowf, vals, old, offs, offs2, offs3, offs4, out_0, out_1, out_2
):
    nc = tc.nc
    with ExitStack() as ctx:
        sbuf = ctx.enter_context(tc.tile_pool(name="sbuf", bufs=1))
        psum = ctx.enter_context(tc.psum_pool(name="psum", bufs=1))

        def tile(name, shape, dtype, in_place_of=None):
            return sbuf.tile(shape, dtype, name=name, tag=in_place_of or name, align_bytes=64)

        def product_bank(columns):
            return psum.tile([P, columns], F32, name="product", tag="product", bufs=PRODUCT_BANKS)

        def scalar_indirect(out, in_):
            nc.scalar.activation(out, in_, COPY)

        def weave(copy, woven, rows):
            copy(woven.rearrange("p (c i) t -> p c t i", i=RUN), rows.rearrange("p t (c i) -> p c t i", i=RUN))

        def quantize(codes, scales, woven):
            nc.vector.quantize_mx(out=codes.bitcast(FP8X4), scales=scales, in_=woven)

        def multiply(out, stationary, stationary_scales, codes, scales):
            nc.tensor.matmul_mx(
                out=out,
                lhsT=stationary,
                lhsT_scale=stationary_scales,
                rhs=codes.bitcast(FP8X4),
                rhs_scale=scales,
                start=True,
                stop=True,
            )

        idx = tile("idx", [P, I // PER_COLUMN], U16)
        idx2 = tile("idx2", [P, J // PER_COLUMN], U16)
        idx3 = tile("idx3", [P, J // PER_COLUMN], U16)
        idx4 = tile("idx4", [P, J // PER_COLUMN], U16)
        key_words = tile("key_words", [P, T], U16)
        key_scales = tile("key_scales", [P, T], U8)
        chunks = U // CHUNK
        notes_rows = [tile("notes_rows%d" % c, [P, PLACES, CHUNK], F32) for c in range(chunks)]
        row_factor = tile("row_factor", [P, PLACES], F32)
        vals_rows = [tile("vals_rows%d" % r, [P, T], F32) for r in range(PLACES)]
        old_rows = [tile("old_rows%d" % r, [P, M], F32) for r in range(PLACES)]
        notes_dealt = notes.rearrange("(p t) u -> p t u", t=PLACES)
        vals_dealt = vals.rearrange("(p r) t -> r p t", r=PLACES)
        old_dealt = old.rearrange("(p r) m -> r p m", r=PLACES)
        out_dealt = out_0.rearrange("(p r) m -> r p m", r=PLACES)

        nc.gpsimd.memset(key_scales[:].bitcast(I32), 0)
        nc.sync.dma_start(idx[:], offs)
        nc.sync.dma_start(key_words[:].bitcast(I32), keys_words[0].bitcast(I32))
        nc.sync.dma_start(notes_rows[0][:], notes_dealt[:, :, :CHUNK])
        for q in range(QUADRANTS):
            nc.sync.dma_start(
                key_scales[32 * q : 32 * q + 4, :].bitcast(I32), keys_scales[0, 4 * q : 4 * q + 4, :].bitcast(I32)
            )
        for c in range(1, chunks):
            nc.sync.dma_start(notes_rows[c][:], notes_dealt[:, :, CHUNK * c : CHUNK * (c + 1)])
        nc.sync.dma_start(idx3[:], offs3)
        nc.sync.dma_start(idx2[:], offs2)
        nc.sync.dma_start(row_factor[:], rowf.rearrange("(p t) o -> p (t o)", t=PLACES))
        nc.sync.dma_start(vals_rows[0][:], vals_dealt[0])
        nc.sync.dma_start(idx4[:], offs4)
        for r in range(1, PLACES):
            nc.sync.dma_start(vals_rows[r][:], vals_dealt[r])
        for r in range(PLACES):
            nc.sync.dma_start(old_rows[r][:], old_dealt[r])

        placed = [tile("placed%d" % r, [P, M], F32) for r in range(PLACES)]
        for r in range(PLACES - 1):
            nc.vector.memset(placed[r][:], 0.0)
        nc.gpsimd.memset(placed[PLACES - 1][:], 0.0)
        identity = tile("identity", [P, P], F32)
        make_identity(nc, identity[:])

        words_listed = tile("words_listed", [P, I], U16)
        words_dealt = tile("words_dealt", [P, 2 * I], U8)
        scales_dealt = tile("scales_dealt", [P, I], U8)
        nc.vector.tensor_copy(words_listed[:], key_words[:].indirect(idx[:]))
        nc.vector.tensor_copy(scales_dealt[:].rearrange("p (t m) -> p m t", t=PLACES), key_scales[:].indirect(idx[:]))
        nc.vector.tensor_copy(
            words_dealt[:].bitcast(U16).rearrange("p (t m) -> p t m", t=PLACES),
            words_listed[:].rearrange("p (m t) -> p t m", t=PLACES),
        )

        notes_codes = [tile("notes_codes%d" % c, [P, CHUNK], U32) for c in range(chunks)]
        notes_scales = [tile("notes_scales%d" % c, [P, CHUNK], U8) for c in range(chunks)]
        for c in range(chunks):
            notes_woven = tile("notes_woven%d" % c, [P, CHUNK, PLACES], BF16)
            weave(nc.scalar.copy if c < chunks // 2 else nc.vector.tensor_copy, notes_woven[:], notes_rows[c][:])
            quantize(notes_codes[c][:], notes_scales[c][:], notes_woven[:].rearrange("p c t -> p (c t)"))

        g1 = [tile("g1_%d" % t, [P, U], F32) for t in range(PLACES)]
        score_banks = {}

        def score(t):
            for side in range(U // BANK):
                score_banks[t, side] = product_bank(BANK)
            for c in range(chunks):
                side, first = divmod(CHUNK * c, BANK)
                multiply(
                    score_banks[t, side][:, first : first + CHUNK],
                    words_dealt[:, 2 * P * t : 2 * P * (t + 1)].bitcast(FP4X4),
                    scales_dealt[:, P * t : P * (t + 1)],
                    notes_codes[c][:],
                    notes_scales[c][:],
                )

        def empty(copy, t, side):
            copy(g1[t][:, BANK * side : BANK * (side + 1)], score_banks[t, side][:])

        for t in range(PLACES - 1):
            score(t)
        for t in range(PLACES - 1):
            empty(nc.scalar.copy, t, 0)
        for t in range(2):
            empty(nc.scalar.copy, t, 1)
        score(PLACES - 1)
        for t, side in ((2, 1), (3, 0), (3, 1)):
            empty(nc.vector.tensor_copy, t, side)

        turned = [psum.tile([P, 2, 2, P], F32, name="turned%d" % g) for g in range(PLACES // 2)]

        def look_up_values(copy, r):
            vals_listed = tile("vals_listed%d" % r, [P, I], BF16)
            copy(vals_listed[:], vals_rows[r][:].indirect(idx[:]))
            for u in range(2):
                nc.tensor.transpose(turned[r // 2][:, r % 2, u, :], vals_listed[:].bitcast(F32)[:, u::2], identity[:])

        subtrahend = [tile("subtrahend%d" % t, [P, J], F32) for t in range(PLACES)]
        for t in range(PLACES):
            scalar_indirect(subtrahend[t][:], g1[t][:].indirect(idx3[:]))
        look_up_values(nc.vector.tensor_copy, 0)
        difference = tile("difference", [P, PLACES, J], F32, in_place_of="vals_rows0")
        table = tile("table", [P, PLACES, J], BF16)

        def subtract(t):
            nc.vector.tensor_tensor(difference[:, t, :], g1[t][:].indirect(idx2[:]), subtrahend[t][:], ALU.subtract)

        def weigh(t):
            nc.vector.tensor_scalar(table[:, t, :], difference[:, t, :], 0.0, row_factor[:, t : t + 1], ALU.max, ALU.mult)

        subtract(0)
        for t in range(1, PLACES):
            subtract(t)
            weigh(t - 1)
        weigh(PLACES - 1)
        for r in range(1, PLACES):
            look_up_values(scalar_indirect, r)

        table_codes = [tile("table_codes%d" % h, [P, HALF], U32) for h in range(2)]
        table_scales = [tile("table_scales%d" % h, [P, HALF], U8) for h in range(2)]
        first_woven = tile("first_woven", [P, HALF, PLACES], BF16)
        weave(nc.vector.tensor_copy, first_woven[:], table[:, :, :HALF])
        quantize(table_codes[0][:], table_scales[0][:], first_woven[:].rearrange("p c t -> p (c t)"))

        vals_woven = tile("vals_woven", [P, PLACES // 2, 2 * P * PLACES], BF16, in_place_of="vals_rows3")
        for g in range(PLACES // 2):
            nc.scalar.copy(
                vals_woven[:, g, :].bitcast(F32).rearrange("p (r m u) -> p r m u", r=2, u=2),
                turned[g][:].rearrange("p r u m -> p r m u"),
            )
        second_woven = tile("second_woven", [P, HALF, PLACES], BF16, in_place_of="vals_listed3")
        weave(nc.scalar.copy, second_woven[:], table[:, :, HALF:])
        vals_codes = tile("vals_codes", [P, E], U32)
        vals_scales = tile("vals_scales", [P, E], U8)
        quantize(vals_codes[:], vals_scales[:], vals_woven[:].rearrange("p g k -> p (g k)"))

        sum_banks = {}

        def product(r, h):
            if r < 2:
                sum_banks[r, h] = product_bank(HALF)
                target = sum_banks[r, h][:]
            else:
                if h == 0:
                    sum_banks[r] = product_bank(J)
                target = sum_banks[r][:, HALF * h : HALF * (h + 1)]
            multiply(
                target,
                vals_codes[:, P * r : P * (r + 1)].bitcast(FP8X4),
                vals_scales[:, P * r : P * (r + 1)],
                table_codes[h][:],
                table_scales[h][:],
            )

        for r in range(PLACES):
            product(r, 0)
        quantize(table_codes[1][:], table_scales[1][:], second_woven[:].rearrange("p c t -> p (c t)"))
        for r in range(PLACES):
            product(r, 1)

        o = [tile("o%d" % r, [P, J], F32) for r in range(PLACES)]
        result = tile("result", [P, PLACES, M], F32)

        def scatter(copy, r, first, last):
            copy(placed[r][:].indirect(idx4[:, first // PER_COLUMN : last // PER_COLUMN]), o[r][:, first:last])

        def add(r, first, last):
            nc.vector.tensor_tensor(result[:, r, first:last], old_rows[r][:, first:last], placed[r][:, first:last], ALU.add)

        def store(r):
            nc.sync.dma_start(out_dealt[r], result[:, r, :])

        nc.vector.tensor_copy(o[0][:, :HALF], sum_banks[0, 0][:])
        scatter(nc.vector.tensor_copy, 0, 0, HALF)
        nc.scalar.copy(o[1][:, :HALF], sum_banks[1, 0][:])
        scatter(scalar_indirect, 1, 0, HALF)
        nc.vector.tensor_copy(o[0][:, HALF:], sum_banks[0, 1][:])
        scatter(nc.vector.tensor_copy, 0, HALF, J)
        nc.scalar.copy(o[1][:, HALF:], sum_banks[1, 1][:])
        nc.scalar.copy(o[2][:], sum_banks[2][:])
        scatter(scalar_indirect, 1, HALF, J)
        scatter(scalar_indirect, 2, 0, SCALAR_ENTRIES)
        add(0, 0, M)
        store(0)
        add(1, 0, M // 2)
        scatter(nc.vector.tensor_copy, 2, SCALAR_ENTRIES, J)
        add(1, M // 2, M)
        store(1)
        nc.scalar.copy(o[3][:], sum_banks[3][:])
        for h in range(2):
            scatter(scalar_indirect, 3, HALF * h, HALF * (h + 1))
        add(2, 0, M)
        store(2)

        out_woven = tile("out_woven", [P, M, PLACES], BF16)
        out_codes = tile("out_codes", [P, M], U32)
        out_scales = tile("out_scales", [P, M], U8)
        words_out = out_1[0].rearrange("p c r -> p (c r)").bitcast(I32)

        def weave_result(copy, quarter):
            columns = slice(QUARTER * quarter, QUARTER * (quarter + 1))
            weave(copy, out_woven[:, columns, :], result[:, :, columns])

        def hand_on(first, last):
            quantize(out_codes[:, first:last], out_scales[:, first:last], out_woven[:, first:last, :].rearrange("p c t -> p (c t)"))
            nc.sync.dma_start(words_out[:, first:last], out_codes[:, first:last].bitcast(I32))

        add(3, 0, QUARTER)
        weave_result(nc.scalar.copy, 0)
        add(3, QUARTER, M)
        store(3)
        weave_result(nc.vector.tensor_copy, 1)
        hand_on(0, 2 * QUARTER)
        weave_result(nc.scalar.copy, 2)
        weave_result(nc.vector.tensor_copy, 3)
        hand_on(2 * QUARTER, 3 * QUARTER)
        hand_on(3 * QUARTER, M)
        for q in range(QUADRANTS):
            queue = nc.sync if q % 2 == 0 else nc.scalar
            queue.dma_start(out_2[0, 4 * q : 4 * q + 4, :].bitcast(I32), out_scales[32 * q : 32 * q + 4, :].bitcast(I32))
